import numpy as np
import ml_dtypes


def mxq(x, axis, fmt="e4m3"):
    dtype, down = {"e4m3": (ml_dtypes.float8_e4m3fn, 7), "e5m2": (ml_dtypes.float8_e5m2, 14)}[fmt]
    v = np.moveaxis(np.asarray(x, np.float32).astype(ml_dtypes.bfloat16).astype(np.float64), axis, -1)
    blocks = v.reshape(v.shape[:-1] + (-1, 32))
    amax = np.abs(blocks).max(-1, keepdims=True)
    byte = np.maximum(np.where(amax > 0, np.frexp(amax)[1] - 1 + 127, 0) - down, 1)
    scale = np.exp2(byte - 127.0)
    codes = (blocks / scale).astype(np.float32).astype(dtype).astype(np.float64)
    return np.moveaxis((codes * scale).reshape(v.shape), -1, axis)


WIDE = False


def mx_kscale(k):
    if not WIDE:
        return np.ones(k)
    levels = np.array([10, -10, 5, -5, 0])
    if k % 512:
        return np.exp2(np.random.permutation(np.resize(levels, k // 32))).repeat(32)
    a = np.empty((k // 512, 16))
    for p in range(k // 512):
        a[p, :8] = np.random.permutation(np.resize(levels, 8))
        for g in range(8):
            far = levels[np.abs(levels - a[p, g]) >= 10]
            a[p, g + 8] = far[np.random.randint(len(far))]
    return np.exp2(a.ravel()).repeat(32)


def f64(x):
    return np.asarray(x).astype(np.float64)


def striped(idx):
    return np.tile(idx.reshape(-1, 16).T, (8, 1)).astype(np.uint16)


def unstriped(offs):
    return offs[:16].T.reshape(-1).astype(np.int64)


def silu(v):
    return v / (1.0 + np.exp(-np.maximum(v, -700.0)))


K, T, E, C, N = 512, 2048, 6, 256, 384


def by_expert(wq, xq):
    return np.concatenate([wq[e].T @ xq[:, e * C:(e + 1) * C] for e in range(E)], axis=1)


def setup_inputs():
    n = np.random.standard_normal
    s = mx_kscale(K)[:, None]
    return {
        "xT": (n((K, T)) * s).astype(np.float32),
        "w": (n((E, K, N)) / np.sqrt(K) / s[None]).astype(np.float32),
        "b": (0.3 * n((N, E))).astype(np.float32),
        "gate": np.tile(np.random.uniform(0.2, 1.0, E * C), (N, 1)).astype(np.float32),
        "offs": striped(np.random.permutation(T)[:E * C]),
    }


def reference(xT, w, b, gate, offs):
    idx = unstriped(offs)
    xq = mxq(f64(xT)[:, idx], 0, "e4m3")
    y = by_expert(mxq(f64(w), 1, "e4m3"), xq)
    y = silu(y + np.repeat(f64(b), C, axis=1))
    out = np.zeros((N, T))
    out[:, idx] = f64(gate) * y
    return out

@@ -1,0 +1,134 @@
+from contextlib import ExitStack
+
+import concourse.mybir as mybir
+
+K, T, E, C, N = 512, 2048, 6, 256, 384
+FLOPS = 2 * K * N * E * C
+BYTES = 4 * (K * T + E * K * N + N * E + 128 * E * C + N * T) + 2 * 128 * E * C // 16
+
+F32 = mybir.dt.float32
+BF16 = mybir.dt.bfloat16
+U32 = mybir.dt.uint32
+I32 = mybir.dt.int32
+U16 = mybir.dt.uint16
+U8 = mybir.dt.uint8
+FP8X4 = mybir.dt.float8_e4m3fn_x4
+MULT = mybir.AluOpType.mult
+SILU = mybir.ActivationFunctionType.Silu
+
+P = 128
+PACK = 4
+M_TILES = N // P
+PAIRS = E // 2
+SLOTS = 2 * C
+LIST = SLOTS // 16
+X_CHUNKS = ((0, 512), (512, 512), (1024, 512), (1536, 256), (1792, 256))
+
+
+def interleave(copy, grouped, raw):
+    copy(
+        out=grouped[:].rearrange("p (c i) j -> p c j i", i=4),
+        in_=raw.rearrange("p j (c i) -> p c j i", i=4),
+    )
+
+
+def tile_routed_moe_kernel(tc, xT, w, b, gate, offs, out):
+    nc = tc.nc
+    with ExitStack() as ctx:
+        keep = ctx.enter_context(tc.tile_pool(name="keep", bufs=1))
+        work = ctx.enter_context(tc.tile_pool(name="work", bufs=4))
+        psum = ctx.enter_context(tc.psum_pool(name="psum", bufs=8))
+
+        offsets = keep.tile([P, E * C // 16], U16, name="offsets")
+        words = keep.tile([P, T], U32, name="words", align_bytes=64)
+        tbytes = keep.tile([P, T], U8, name="tbytes", align_bytes=64)
+        bias = keep.tile([P, M_TILES, E], F32, name="bias")
+        gates = keep.tile([P, E * C], F32, name="gates")
+        windows = [keep.tile([P, T], F32, name=f"window{m}") for m in range(M_TILES)]
+        warm = keep.tile([P, 1], F32, name="warm")
+
+        xv = xT.rearrange("(p j) t -> p j t", j=PACK)
+        x_raw = []
+        for i, (t0, n) in enumerate(X_CHUNKS):
+            raw = keep.tile([P, PACK, n], F32, name=f"x_raw{i}")
+            nc.sync.dma_start(out=raw[:], in_=xv[:, :, t0 : t0 + n])
+            x_raw.append(raw)
+            if i == 1:
+                nc.sync.dma_start(offsets[:], offs)
+        w_raw = []
+        for e in range(E):
+            raw = keep.tile([P, PACK, N], F32, name=f"w_raw{e}")
+            nc.sync.dma_start(out=raw[:], in_=w[e].rearrange("(p j) n -> p j n", j=PACK))
+            w_raw.append(raw)
+            if e == 0:
+                nc.sync.dma_start(out=bias[:], in_=b.rearrange("(m p) e -> p m e", p=P))
+            if e == 1:
+                nc.sync.dma_start(out=gates[:], in_=gate[0:P, :])
+
+        nc.vector.memset(warm[:], 0.0)
+        nc.scalar.activation(out=warm[:], in_=warm[:], func=SILU)
+        nc.gpsimd.memset(tbytes[:].bitcast(I32), 0)
+        nc.vector.memset(windows[0][:], 0.0)
+        nc.vector.memset(windows[1][:], 0.0)
+        nc.gpsimd.memset(windows[2][:], 0.0)
+
+        for i, (t0, n) in enumerate(X_CHUNKS):
+            grouped = keep.tile([P, n, PACK], BF16, name=f"x_grouped{i}", align_bytes=64)
+            interleave(nc.scalar.copy if i == 3 else nc.vector.tensor_copy, grouped, x_raw[i][:])
+            nc.vector.quantize_mx(
+                out=words[:, t0 : t0 + n].bitcast(FP8X4),
+                scales=tbytes[:, t0 : t0 + n],
+                in_=grouped[:].rearrange("p t j -> p (t j)"),
+            )
+
+        slot_words, slot_bytes = [], []
+        for q in range(PAIRS):
+            listed = offsets[:, q * LIST : (q + 1) * LIST]
+            sw = keep.tile([P, SLOTS], U32, name=f"slot_words{q}", align_bytes=64)
+            sb = keep.tile([P, SLOTS], U8, name=f"slot_bytes{q}", align_bytes=64)
+            nc.vector.tensor_copy(out=sw[:], in_=words[:].indirect(listed))
+            nc.vector.tensor_copy(out=sb[:], in_=tbytes[:].indirect(listed))
+            slot_words.append(sw)
+            slot_bytes.append(sb)
+
+        w_codes, w_bytes = [], []
+        for q in range(PAIRS):
+            grouped = keep.tile([P, 2 * N, PACK], BF16, name=f"w_grouped{q}", align_bytes=64)
+            for h in range(2):
+                nc.scalar.copy(
+                    out=grouped[:, h * N : (h + 1) * N, :].rearrange("p (c i) j -> p c j i", i=4),
+                    in_=w_raw[2 * q + h][:].rearrange("p j (c i) -> p c j i", i=4),
+                )
+            wc = keep.tile([P, 2 * N], U32, name=f"w_codes{q}", align_bytes=64)
+            wb = keep.tile([P, 2 * N], U8, name=f"w_bytes{q}", align_bytes=64)
+            for c0, n in ((0, 512), (512, 256)):
+                nc.vector.quantize_mx(
+                    out=wc[:, c0 : c0 + n].bitcast(FP8X4),
+                    scales=wb[:, c0 : c0 + n],
+                    in_=grouped[:, c0 : c0 + n, :].rearrange("p n j -> p (n j)"),
+                )
+            w_codes.append(wc)
+            w_bytes.append(wb)
+
+        for m in range(M_TILES):
+            for q in range(PAIRS):
+                acc = psum.tile([P, SLOTS], F32, name="acc")
+                y = work.tile([P, SLOTS], F32, name="y")
+                for h in range(2):
+                    cols = slice(h * C, (h + 1) * C)
+                    feats = slice(h * N + m * P, h * N + (m + 1) * P)
+                    nc.tensor.matmul_mx(
+                        out=acc[:, cols],
+                        lhsT=w_codes[q][:, feats].bitcast(FP8X4),
+                        lhsT_scale=w_bytes[q][:, feats],
+                        rhs=slot_words[q][:, cols].bitcast(FP8X4),
+                        rhs_scale=slot_bytes[q][:, cols],
+                        start=True,
+                        stop=True,
+                    )
+                    e = 2 * q + h
+                    nc.scalar.activation(out=y[:, cols], in_=acc[:, cols], func=SILU, bias=bias[:, m, e : e + 1])
+                gy = work.tile([P, SLOTS], F32, name="gy")
+                nc.vector.tensor_tensor(out=gy[:], in0=y[:], in1=gates[:, q * SLOTS : (q + 1) * SLOTS], op=MULT)
+                nc.vector.tensor_copy(out=windows[m][:].indirect(offsets[:, q * LIST : (q + 1) * LIST]), in_=gy[:])
+            nc.sync.dma_start(out=out[m * P : (m + 1) * P, :], in_=windows[m][:])

@@ -19,17 +19,10 @@ SILU = mybir.ActivationFunctionType.Silu
 P = 128
 PACK = 4
 M_TILES = N // P
-PAIRS = E // 2
-SLOTS = 2 * C
-LIST = SLOTS // 16
-X_CHUNKS = ((0, 512), (512, 512), (1024, 512), (1536, 256), (1792, 256))
-
-
-def interleave(copy, grouped, raw):
-    copy(
-        out=grouped[:].rearrange("p (c i) j -> p c j i", i=4),
-        in_=raw.rearrange("p j (c i) -> p c j i", i=4),
-    )
+CHUNKS = ((0, 1024), (1024, 2048))
+LATE_CHUNKS = ((0, 1024), (1024, 1536), (1536, 2048))
+UNITS = ((0,), (1,), (2,), (3,), (4, 5))
+COPY = mybir.ActivationFunctionType.Copy
 
 
 def tile_routed_moe_kernel(tc, xT, w, b, gate, offs, out):
@@ -40,95 +33,117 @@ def tile_routed_moe_kernel(tc, xT, w, b, gate, offs, out):
         psum = ctx.enter_context(tc.psum_pool(name="psum", bufs=8))
 
         offsets = keep.tile([P, E * C // 16], U16, name="offsets")
-        words = keep.tile([P, T], U32, name="words", align_bytes=64)
-        tbytes = keep.tile([P, T], U8, name="tbytes", align_bytes=64)
         bias = keep.tile([P, M_TILES, E], F32, name="bias")
-        gates = keep.tile([P, E * C], F32, name="gates")
+        gate_first = keep.tile([P, C], F32, name="gate_first")
+        gate_rest = keep.tile([P, (E - 1) * C], F32, name="gate_rest")
         windows = [keep.tile([P, T], F32, name=f"window{m}") for m in range(M_TILES)]
         warm = keep.tile([P, 1], F32, name="warm")
 
         xv = xT.rearrange("(p j) t -> p j t", j=PACK)
-        x_raw = []
-        for i, (t0, n) in enumerate(X_CHUNKS):
-            raw = keep.tile([P, PACK, n], F32, name=f"x_raw{i}")
-            nc.sync.dma_start(out=raw[:], in_=xv[:, :, t0 : t0 + n])
-            x_raw.append(raw)
-            if i == 1:
+        early = keep.tile([P, T, 2], BF16, name="early", align_bytes=64)
+        late = keep.tile([P, 2, T], BF16, name="late", align_bytes=64)
+        late_raw = keep.tile([P, 2, T], F32, name="late_raw")
+        early_raw = []
+        for c, (t0, t1) in enumerate(CHUNKS):
+            raw = keep.tile([P, 2, t1 - t0], F32, name=f"early_raw{c}")
+            nc.sync.dma_start(out=raw[:], in_=xv[:, 0:2, t0:t1])
+            early_raw.append(raw)
+            if c == 0:
                 nc.sync.dma_start(offsets[:], offs)
+        for t0, t1 in LATE_CHUNKS:
+            nc.sync.dma_start(out=late_raw[:, :, t0:t1], in_=xv[:, 2:4, t0:t1])
         w_raw = []
         for e in range(E):
             raw = keep.tile([P, PACK, N], F32, name=f"w_raw{e}")
-            nc.sync.dma_start(out=raw[:], in_=w[e].rearrange("(p j) n -> p j n", j=PACK))
+            wv = w[e].rearrange("(p j) n -> p j n", j=PACK)
+            if e == 0:
+                nc.sync.dma_start(out=raw[:, :, 0:P], in_=wv[:, :, 0:P])
+                nc.sync.dma_start(out=raw[:, :, P:], in_=wv[:, :, P:])
+            else:
+                nc.sync.dma_start(out=raw[:], in_=wv)
             w_raw.append(raw)
             if e == 0:
                 nc.sync.dma_start(out=bias[:], in_=b.rearrange("(m p) e -> p m e", p=P))
+                nc.sync.dma_start(out=gate_first[:], in_=gate[0:P, 0:C])
             if e == 1:
-                nc.sync.dma_start(out=gates[:], in_=gate[0:P, :])
+                nc.sync.dma_start(out=gate_rest[:], in_=gate[0:P, C:])
 
         nc.vector.memset(warm[:], 0.0)
         nc.scalar.activation(out=warm[:], in_=warm[:], func=SILU)
-        nc.gpsimd.memset(tbytes[:].bitcast(I32), 0)
         nc.vector.memset(windows[0][:], 0.0)
         nc.vector.memset(windows[1][:], 0.0)
         nc.gpsimd.memset(windows[2][:], 0.0)
 
-        for i, (t0, n) in enumerate(X_CHUNKS):
-            grouped = keep.tile([P, n, PACK], BF16, name=f"x_grouped{i}", align_bytes=64)
-            interleave(nc.scalar.copy if i == 3 else nc.vector.tensor_copy, grouped, x_raw[i][:])
-            nc.vector.quantize_mx(
-                out=words[:, t0 : t0 + n].bitcast(FP8X4),
-                scales=tbytes[:, t0 : t0 + n],
-                in_=grouped[:].rearrange("p t j -> p (t j)"),
+        for (t0, t1), raw in zip(CHUNKS, early_raw):
+            nc.vector.tensor_copy(
+                out=early[:, t0:t1, :].rearrange("p (c i) u -> p c u i", i=4),
+                in_=raw[:].rearrange("p u (c i) -> p c u i", i=4),
             )
+        early_words = early[:].rearrange("p t u -> p (t u)").bitcast(U32)
+        grouped = []
+        for u, experts in enumerate(UNITS):
+            slots = len(experts) * C
+            first = experts[0] * C // 16
+            g = keep.tile([P, slots, PACK], BF16, name=f"grouped{u}", align_bytes=64)
+            nc.vector.tensor_copy(
+                out=g[:].rearrange("p n j -> p (n j)").bitcast(U32).rearrange("p (n u) -> p n u", u=2)[:, :, 0],
+                in_=early_words.indirect(offsets[:, first : first + slots // 16]),
+            )
+            grouped.append(g)
+        for t0, t1 in LATE_CHUNKS:
+            nc.scalar.copy(out=late[:, :, t0:t1], in_=late_raw[:, :, t0:t1])
 
-        slot_words, slot_bytes = [], []
-        for q in range(PAIRS):
-            listed = offsets[:, q * LIST : (q + 1) * LIST]
-            sw = keep.tile([P, SLOTS], U32, name=f"slot_words{q}", align_bytes=64)
-            sb = keep.tile([P, SLOTS], U8, name=f"slot_bytes{q}", align_bytes=64)
-            nc.vector.tensor_copy(out=sw[:], in_=words[:].indirect(listed))
-            nc.vector.tensor_copy(out=sb[:], in_=tbytes[:].indirect(listed))
-            slot_words.append(sw)
-            slot_bytes.append(sb)
+        for u, experts in enumerate(UNITS):
+            count = len(experts)
+            slots = count * C
+            first = experts[0] * C // 16
+            listed = offsets[:, first : first + slots // 16]
+            g = grouped[u]
+            for t in range(2):
+                if u == 0:
+                    nc.vector.tensor_copy(out=g[:, :, 2 + t], in_=late_raw[:, t, :].indirect(listed))
+                else:
+                    nc.scalar.activation(out=g[:, :, 2 + t], in_=late[:, t, :].indirect(listed), func=COPY)
+            xc = keep.tile([P, slots], U32, name=f"x_codes{u}", align_bytes=64)
+            xb = keep.tile([P, slots], U8, name=f"x_bytes{u}", align_bytes=64)
+            nc.vector.quantize_mx(out=xc[:].bitcast(FP8X4), scales=xb[:], in_=g[:].rearrange("p n j -> p (n j)"))
 
-        w_codes, w_bytes = [], []
-        for q in range(PAIRS):
-            grouped = keep.tile([P, 2 * N, PACK], BF16, name=f"w_grouped{q}", align_bytes=64)
-            for h in range(2):
-                nc.scalar.copy(
-                    out=grouped[:, h * N : (h + 1) * N, :].rearrange("p (c i) j -> p c j i", i=4),
-                    in_=w_raw[2 * q + h][:].rearrange("p j (c i) -> p c j i", i=4),
+            wg = keep.tile([P, count * N, PACK], BF16, name=f"w_grouped{u}", align_bytes=64)
+            for h, e, n0, n1 in ((0, 0, 0, P), (0, 0, P, N)) if u == 0 else [(h, e, 0, N) for h, e in enumerate(experts)]:
+                copy = nc.vector.tensor_copy if e in (0, 1) else nc.scalar.copy
+                copy(
+                    out=wg[:, h * N + n0 : h * N + n1, :].rearrange("p (c i) j -> p c j i", i=4),
+                    in_=w_raw[e][:, :, n0:n1].rearrange("p j (c i) -> p c j i", i=4),
                 )
-            wc = keep.tile([P, 2 * N], U32, name=f"w_codes{q}", align_bytes=64)
-            wb = keep.tile([P, 2 * N], U8, name=f"w_bytes{q}", align_bytes=64)
-            for c0, n in ((0, 512), (512, 256)):
+            wc = keep.tile([P, count * N], U32, name=f"w_codes{u}", align_bytes=64)
+            wb = keep.tile([P, count * N], U8, name=f"w_bytes{u}", align_bytes=64)
+            for c0, n in ((0, P), (P, 2 * P)) if u == 0 else ((0, count * 256), (count * 256, count * 128)):
                 nc.vector.quantize_mx(
                     out=wc[:, c0 : c0 + n].bitcast(FP8X4),
                     scales=wb[:, c0 : c0 + n],
-                    in_=grouped[:, c0 : c0 + n, :].rearrange("p n j -> p (n j)"),
+                    in_=wg[:, c0 : c0 + n, :].rearrange("p n j -> p (n j)"),
                 )
-            w_codes.append(wc)
-            w_bytes.append(wb)
-
-        for m in range(M_TILES):
-            for q in range(PAIRS):
-                acc = psum.tile([P, SLOTS], F32, name="acc")
-                y = work.tile([P, SLOTS], F32, name="y")
-                for h in range(2):
+            for m in range(M_TILES):
+                acc = psum.tile([P, 512], F32, name="acc")
+                y = work.tile([P, 512], F32, name="y")
+                for h, e in enumerate(experts):
                     cols = slice(h * C, (h + 1) * C)
                     feats = slice(h * N + m * P, h * N + (m + 1) * P)
                     nc.tensor.matmul_mx(
                         out=acc[:, cols],
-                        lhsT=w_codes[q][:, feats].bitcast(FP8X4),
-                        lhsT_scale=w_bytes[q][:, feats],
-                        rhs=slot_words[q][:, cols].bitcast(FP8X4),
-                        rhs_scale=slot_bytes[q][:, cols],
+                        lhsT=wc[:, feats].bitcast(FP8X4),
+                        lhsT_scale=wb[:, feats],
+                        rhs=xc[:, cols].bitcast(FP8X4),
+                        rhs_scale=xb[:, cols],
                         start=True,
                         stop=True,
                     )
-                    e = 2 * q + h
                     nc.scalar.activation(out=y[:, cols], in_=acc[:, cols], func=SILU, bias=bias[:, m, e : e + 1])
-                gy = work.tile([P, SLOTS], F32, name="gy")
-                nc.vector.tensor_tensor(out=gy[:], in0=y[:], in1=gates[:, q * SLOTS : (q + 1) * SLOTS], op=MULT)
-                nc.vector.tensor_copy(out=windows[m][:].indirect(offsets[:, q * LIST : (q + 1) * LIST]), in_=gy[:])
-            nc.sync.dma_start(out=out[m * P : (m + 1) * P, :], in_=windows[m][:])
+                nc.vector.tensor_tensor(
+                    out=windows[m][:].indirect(listed),
+                    in0=y[:, 0:slots],
+                    in1=gate_first[:] if u == 0 else gate_rest[:, experts[0] * C - C : experts[0] * C - C + slots],
+                    op=MULT,
+                )
+                if u == len(UNITS) - 1:
+                    nc.sync.dma_start(out=out[m * P : (m + 1) * P, :], in_=windows[m][:])

@@ -19,14 +19,22 @@ SILU = mybir.ActivationFunctionType.Silu
 P = 128
 PACK = 4
 M_TILES = N // P
-CHUNKS = ((0, 1024), (1024, 2048))
-LATE_CHUNKS = ((0, 1024), (1024, 1536), (1536, 2048))
 UNITS = ((0,), (1,), (2,), (3,), (4, 5))
+EARLY = ((0, 1024), (1024, 1536), (1536, 2048))
+LATE = ((0, 512), (512, 1024), (1024, 1536), (1536, 2048))
+PUN = ((0, 6),)
 COPY = mybir.ActivationFunctionType.Copy
+
+
+def interleave(copy, out, raw):
+    copy(out=out.rearrange("p (c i) j -> p c j i", i=4), in_=raw.rearrange("p j (c i) -> p c j i", i=4))
 
 
 def tile_routed_moe_kernel(tc, xT, w, b, gate, offs, out):
     nc = tc.nc
+    early_copy = (nc.vector.tensor_copy, nc.vector.tensor_copy, nc.vector.tensor_copy,)
+    late_copy = (nc.scalar.copy, nc.scalar.copy, nc.scalar.copy, nc.vector.tensor_copy,)
+    w_copy = (nc.scalar.copy, nc.vector.tensor_copy, nc.scalar.copy, nc.scalar.copy, nc.scalar.copy, nc.scalar.copy,)
     with ExitStack() as ctx:
         keep = ctx.enter_context(tc.tile_pool(name="keep", bufs=1))
         work = ctx.enter_context(tc.tile_pool(name="work", bufs=4))
@@ -43,28 +51,26 @@ def tile_routed_moe_kernel(tc, xT, w, b, gate, offs, out):
         early = keep.tile([P, T, 2], BF16, name="early", align_bytes=64)
         late = keep.tile([P, 2, T], BF16, name="late", align_bytes=64)
         late_raw = keep.tile([P, 2, T], F32, name="late_raw")
-        early_raw = []
-        for c, (t0, t1) in enumerate(CHUNKS):
+        early_raw, w_raw = [], []
+        for c, (t0, t1) in enumerate(EARLY):
             raw = keep.tile([P, 2, t1 - t0], F32, name=f"early_raw{c}")
             nc.sync.dma_start(out=raw[:], in_=xv[:, 0:2, t0:t1])
             early_raw.append(raw)
             if c == 0:
                 nc.sync.dma_start(offsets[:], offs)
-        for t0, t1 in LATE_CHUNKS:
+        for t0, t1 in LATE:
             nc.sync.dma_start(out=late_raw[:, :, t0:t1], in_=xv[:, 2:4, t0:t1])
-        w_raw = []
         for e in range(E):
             raw = keep.tile([P, PACK, N], F32, name=f"w_raw{e}")
             wv = w[e].rearrange("(p j) n -> p j n", j=PACK)
             if e == 0:
                 nc.sync.dma_start(out=raw[:, :, 0:P], in_=wv[:, :, 0:P])
                 nc.sync.dma_start(out=raw[:, :, P:], in_=wv[:, :, P:])
+                nc.sync.dma_start(out=bias[:], in_=b.rearrange("(m p) e -> p m e", p=P))
+                nc.sync.dma_start(out=gate_first[:], in_=gate[0:P, 0:C])
             else:
                 nc.sync.dma_start(out=raw[:], in_=wv)
             w_raw.append(raw)
-            if e == 0:
-                nc.sync.dma_start(out=bias[:], in_=b.rearrange("(m p) e -> p m e", p=P))
-                nc.sync.dma_start(out=gate_first[:], in_=gate[0:P, 0:C])
             if e == 1:
                 nc.sync.dma_start(out=gate_rest[:], in_=gate[0:P, C:])
 
@@ -74,47 +80,37 @@ def tile_routed_moe_kernel(tc, xT, w, b, gate, offs, out):
         nc.vector.memset(windows[1][:], 0.0)
         nc.gpsimd.memset(windows[2][:], 0.0)
 
-        for (t0, t1), raw in zip(CHUNKS, early_raw):
-            nc.vector.tensor_copy(
-                out=early[:, t0:t1, :].rearrange("p (c i) u -> p c u i", i=4),
-                in_=raw[:].rearrange("p u (c i) -> p c u i", i=4),
-            )
+        for (t0, t1), raw, copy in zip(EARLY, early_raw, early_copy):
+            interleave(copy, early[:, t0:t1, :], raw[:])
         early_words = early[:].rearrange("p t u -> p (t u)").bitcast(U32)
-        grouped = []
-        for u, experts in enumerate(UNITS):
-            slots = len(experts) * C
-            first = experts[0] * C // 16
-            g = keep.tile([P, slots, PACK], BF16, name=f"grouped{u}", align_bytes=64)
+        grouped = keep.tile([P, E * C, PACK], BF16, name="grouped", align_bytes=64)
+        for e0, e1 in PUN:
             nc.vector.tensor_copy(
-                out=g[:].rearrange("p n j -> p (n j)").bitcast(U32).rearrange("p (n u) -> p n u", u=2)[:, :, 0],
-                in_=early_words.indirect(offsets[:, first : first + slots // 16]),
+                out=grouped[:, e0 * C : e1 * C, :].rearrange("p n j -> p (n j)").bitcast(U32).rearrange("p (n u) -> p n u", u=2)[:, :, 0],
+                in_=early_words.indirect(offsets[:, e0 * C // 16 : e1 * C // 16]),
             )
-            grouped.append(g)
-        for t0, t1 in LATE_CHUNKS:
-            nc.scalar.copy(out=late[:, :, t0:t1], in_=late_raw[:, :, t0:t1])
+        for (t0, t1), copy in zip(LATE, late_copy):
+            copy(out=late[:, :, t0:t1], in_=late_raw[:, :, t0:t1])
 
-        for u, experts in enumerate(UNITS):
+        def prepare(u):
+            experts = UNITS[u]
             count = len(experts)
             slots = count * C
-            first = experts[0] * C // 16
-            listed = offsets[:, first : first + slots // 16]
-            g = grouped[u]
-            for t in range(2):
-                if u == 0:
-                    nc.vector.tensor_copy(out=g[:, :, 2 + t], in_=late_raw[:, t, :].indirect(listed))
+            first = experts[0] * C
+            listed = offsets[:, first // 16 : (first + slots) // 16]
+            g = grouped[:, first : first + slots, :]
+            for j in range(2):
+                if u in (0,):
+                    nc.vector.tensor_copy(out=g[:, :, 2 + j], in_=late_raw[:, j, :].indirect(listed))
                 else:
-                    nc.scalar.activation(out=g[:, :, 2 + t], in_=late[:, t, :].indirect(listed), func=COPY)
+                    nc.scalar.activation(out=g[:, :, 2 + j], in_=late[:, j, :].indirect(listed), func=COPY)
             xc = keep.tile([P, slots], U32, name=f"x_codes{u}", align_bytes=64)
             xb = keep.tile([P, slots], U8, name=f"x_bytes{u}", align_bytes=64)
-            nc.vector.quantize_mx(out=xc[:].bitcast(FP8X4), scales=xb[:], in_=g[:].rearrange("p n j -> p (n j)"))
+            nc.vector.quantize_mx(out=xc[:].bitcast(FP8X4), scales=xb[:], in_=g.rearrange("p n j -> p (n j)"))
 
             wg = keep.tile([P, count * N, PACK], BF16, name=f"w_grouped{u}", align_bytes=64)
             for h, e, n0, n1 in ((0, 0, 0, P), (0, 0, P, N)) if u == 0 else [(h, e, 0, N) for h, e in enumerate(experts)]:
-                copy = nc.vector.tensor_copy if e in (0, 1) else nc.scalar.copy
-                copy(
-                    out=wg[:, h * N + n0 : h * N + n1, :].rearrange("p (c i) j -> p c j i", i=4),
-                    in_=w_raw[e][:, :, n0:n1].rearrange("p j (c i) -> p c j i", i=4),
-                )
+                interleave(w_copy[e], wg[:, h * N + n0 : h * N + n1, :], w_raw[e][:, :, n0:n1])
             wc = keep.tile([P, count * N], U32, name=f"w_codes{u}", align_bytes=64)
             wb = keep.tile([P, count * N], U8, name=f"w_bytes{u}", align_bytes=64)
             for c0, n in ((0, P), (P, 2 * P)) if u == 0 else ((0, count * 256), (count * 256, count * 128)):
@@ -123,6 +119,13 @@ def tile_routed_moe_kernel(tc, xT, w, b, gate, offs, out):
                     scales=wb[:, c0 : c0 + n],
                     in_=wg[:, c0 : c0 + n, :].rearrange("p n j -> p (n j)"),
                 )
+            return xc, xb, wc, wb
+
+        def compute(u, xc, xb, wc, wb):
+            experts = UNITS[u]
+            slots = len(experts) * C
+            first = experts[0] * C
+            listed = offsets[:, first // 16 : (first + slots) // 16]
             for m in range(M_TILES):
                 acc = psum.tile([P, 512], F32, name="acc")
                 y = work.tile([P, 512], F32, name="y")
@@ -142,8 +145,14 @@ def tile_routed_moe_kernel(tc, xT, w, b, gate, offs, out):
                 nc.vector.tensor_tensor(
                     out=windows[m][:].indirect(listed),
                     in0=y[:, 0:slots],
-                    in1=gate_first[:] if u == 0 else gate_rest[:, experts[0] * C - C : experts[0] * C - C + slots],
+                    in1=gate_first[:] if u == 0 else gate_rest[:, first - C : first - C + slots],
                     op=MULT,
                 )
                 if u == len(UNITS) - 1:
                     nc.sync.dma_start(out=out[m * P : (m + 1) * P, :], in_=windows[m][:])
+
+        ready = [prepare(0)]
+        for u in range(len(UNITS)):
+            if u + 1 < len(UNITS):
+                ready.append(prepare(u + 1))
+            compute(u, *ready[u])

@@ -21,6 +21,7 @@ PACK = 4
 M_TILES = N // P
 UNITS = ((0,), (1,), (2,), (3,), (4, 5))
 EARLY = ((0, 1024), (1024, 1536), (1536, 2048))
+LATE_LOADS = ((0, 1024), (1024, 2048))
 LATE = ((0, 512), (512, 1024), (1024, 1536), (1536, 2048))
 PUN = ((0, 6),)
 COPY = mybir.ActivationFunctionType.Copy
@@ -58,14 +59,13 @@ def tile_routed_moe_kernel(tc, xT, w, b, gate, offs, out):
             early_raw.append(raw)
             if c == 0:
                 nc.sync.dma_start(offsets[:], offs)
-        for t0, t1 in LATE:
+        for t0, t1 in LATE_LOADS:
             nc.sync.dma_start(out=late_raw[:, :, t0:t1], in_=xv[:, 2:4, t0:t1])
         for e in range(E):
             raw = keep.tile([P, PACK, N], F32, name=f"w_raw{e}")
             wv = w[e].rearrange("(p j) n -> p j n", j=PACK)
             if e == 0:
-                nc.sync.dma_start(out=raw[:, :, 0:P], in_=wv[:, :, 0:P])
-                nc.sync.dma_start(out=raw[:, :, P:], in_=wv[:, :, P:])
+                nc.sync.dma_start(out=raw[:], in_=wv)
                 nc.sync.dma_start(out=bias[:], in_=b.rearrange("(m p) e -> p m e", p=P))
                 nc.sync.dma_start(out=gate_first[:], in_=gate[0:P, 0:C])
             else:

@@ -4,73 +4,74 @@ import concourse.mybir as mybir
 
 K, T, E, C, N = 512, 2048, 6, 256, 384
 FLOPS = 2 * K * N * E * C
-BYTES = 4 * (K * T + E * K * N + N * E + 128 * E * C + N * T) + 2 * 128 * E * C // 16
+BYTES = 4 * (K * T + E * K * N + N * E + E * C + N * T) + 2 * 128 * (E * C // 16)
 
 F32 = mybir.dt.float32
 BF16 = mybir.dt.bfloat16
 U32 = mybir.dt.uint32
-I32 = mybir.dt.int32
 U16 = mybir.dt.uint16
 U8 = mybir.dt.uint8
 FP8X4 = mybir.dt.float8_e4m3fn_x4
 MULT = mybir.AluOpType.mult
 SILU = mybir.ActivationFunctionType.Silu
+COPY = mybir.ActivationFunctionType.Copy
 
 P = 128
 PACK = 4
-M_TILES = N // P
+BLOCKS = N // P
+BANK = 512
+BANKS = 8
+
 UNITS = ((0,), (1,), (2,), (3,), (4, 5))
-EARLY = ((0, 1024), (1024, 1536), (1536, 2048))
-LATE_LOADS = ((0, 1024), (1024, 2048))
-LATE = ((0, 512), (512, 1024), (1024, 1536), (1536, 2048))
-PUN = ((0, 6),)
-COPY = mybir.ActivationFunctionType.Copy
+PAIR_LOADS = ((0, 1024), (1024, 1536), (1536, 2048))
+SINGLE_LOADS = ((0, 1024), (1024, 2048))
+SINGLE_COPIES = ((0, 512), (512, 1024), (1024, 1536), (1536, 2048))
+RESULT_BUFS = 12
 
 
 def interleave(copy, out, raw):
     copy(out=out.rearrange("p (c i) j -> p c j i", i=4), in_=raw.rearrange("p j (c i) -> p c j i", i=4))
 
 
+def flat(tile_view):
+    return tile_view.rearrange("p n j -> p (n j)")
+
+
 def tile_routed_moe_kernel(tc, xT, w, b, gate, offs, out):
     nc = tc.nc
-    early_copy = (nc.vector.tensor_copy, nc.vector.tensor_copy, nc.vector.tensor_copy,)
-    late_copy = (nc.scalar.copy, nc.scalar.copy, nc.scalar.copy, nc.vector.tensor_copy,)
-    w_copy = (nc.scalar.copy, nc.vector.tensor_copy, nc.scalar.copy, nc.scalar.copy, nc.scalar.copy, nc.scalar.copy,)
     with ExitStack() as ctx:
         keep = ctx.enter_context(tc.tile_pool(name="keep", bufs=1))
-        work = ctx.enter_context(tc.tile_pool(name="work", bufs=4))
-        psum = ctx.enter_context(tc.psum_pool(name="psum", bufs=8))
+        results = ctx.enter_context(tc.tile_pool(name="results", bufs=RESULT_BUFS))
+        psum = ctx.enter_context(tc.psum_pool(name="psum", bufs=BANKS))
 
         offsets = keep.tile([P, E * C // 16], U16, name="offsets")
-        bias = keep.tile([P, M_TILES, E], F32, name="bias")
+        bias = keep.tile([P, BLOCKS, E], F32, name="bias")
         gate_first = keep.tile([P, C], F32, name="gate_first")
         gate_rest = keep.tile([P, (E - 1) * C], F32, name="gate_rest")
-        windows = [keep.tile([P, T], F32, name=f"window{m}") for m in range(M_TILES)]
+        windows = [keep.tile([P, T], F32, name=f"window{m}") for m in range(BLOCKS)]
         warm = keep.tile([P, 1], F32, name="warm")
+        pairs = keep.tile([P, T, 2], BF16, name="pairs", align_bytes=64)
+        singles = keep.tile([P, 2, T], BF16, name="singles", align_bytes=64)
+        singles_raw = keep.tile([P, 2, T], F32, name="singles_raw")
+        grouped = keep.tile([P, E * C, PACK], BF16, name="grouped", align_bytes=64)
 
-        xv = xT.rearrange("(p j) t -> p j t", j=PACK)
-        early = keep.tile([P, T, 2], BF16, name="early", align_bytes=64)
-        late = keep.tile([P, 2, T], BF16, name="late", align_bytes=64)
-        late_raw = keep.tile([P, 2, T], F32, name="late_raw")
-        early_raw, w_raw = [], []
-        for c, (t0, t1) in enumerate(EARLY):
-            raw = keep.tile([P, 2, t1 - t0], F32, name=f"early_raw{c}")
-            nc.sync.dma_start(out=raw[:], in_=xv[:, 0:2, t0:t1])
-            early_raw.append(raw)
+        x_rows = xT.rearrange("(p j) t -> p j t", j=PACK)
+        pairs_raw, w_raw = [], []
+        for c, (t0, t1) in enumerate(PAIR_LOADS):
+            raw = keep.tile([P, 2, t1 - t0], F32, name=f"pairs_raw{c}")
+            nc.sync.dma_start(out=raw[:], in_=x_rows[:, 0:2, t0:t1])
+            pairs_raw.append(raw)
             if c == 0:
                 nc.sync.dma_start(offsets[:], offs)
-        for t0, t1 in LATE_LOADS:
-            nc.sync.dma_start(out=late_raw[:, :, t0:t1], in_=xv[:, 2:4, t0:t1])
+        for t0, t1 in SINGLE_LOADS:
+            nc.sync.dma_start(out=singles_raw[:, :, t0:t1], in_=x_rows[:, 2:4, t0:t1])
         for e in range(E):
             raw = keep.tile([P, PACK, N], F32, name=f"w_raw{e}")
-            wv = w[e].rearrange("(p j) n -> p j n", j=PACK)
+            nc.sync.dma_start(out=raw[:], in_=w[e].rearrange("(p j) n -> p j n", j=PACK))
+            w_raw.append(raw)
             if e == 0:
-                nc.sync.dma_start(out=raw[:], in_=wv)
                 nc.sync.dma_start(out=bias[:], in_=b.rearrange("(m p) e -> p m e", p=P))
                 nc.sync.dma_start(out=gate_first[:], in_=gate[0:P, 0:C])
-            else:
-                nc.sync.dma_start(out=raw[:], in_=wv)
-            w_raw.append(raw)
             if e == 1:
                 nc.sync.dma_start(out=gate_rest[:], in_=gate[0:P, C:])
 
@@ -80,79 +81,83 @@ def tile_routed_moe_kernel(tc, xT, w, b, gate, offs, out):
         nc.vector.memset(windows[1][:], 0.0)
         nc.gpsimd.memset(windows[2][:], 0.0)
 
-        for (t0, t1), raw, copy in zip(EARLY, early_raw, early_copy):
-            interleave(copy, early[:, t0:t1, :], raw[:])
-        early_words = early[:].rearrange("p t u -> p (t u)").bitcast(U32)
-        grouped = keep.tile([P, E * C, PACK], BF16, name="grouped", align_bytes=64)
-        for e0, e1 in PUN:
-            nc.vector.tensor_copy(
-                out=grouped[:, e0 * C : e1 * C, :].rearrange("p n j -> p (n j)").bitcast(U32).rearrange("p (n u) -> p n u", u=2)[:, :, 0],
-                in_=early_words.indirect(offsets[:, e0 * C // 16 : e1 * C // 16]),
-            )
-        for (t0, t1), copy in zip(LATE, late_copy):
-            copy(out=late[:, :, t0:t1], in_=late_raw[:, :, t0:t1])
+        for (t0, t1), raw in zip(PAIR_LOADS, pairs_raw):
+            interleave(nc.vector.tensor_copy, pairs[:, t0:t1, :], raw[:])
+        nc.vector.tensor_copy(
+            out=flat(grouped[:]).bitcast(U32).rearrange("p (n u) -> p n u", u=2)[:, :, 0],
+            in_=flat(pairs[:]).bitcast(U32).indirect(offsets[:]),
+        )
+        for t0, t1 in SINGLE_COPIES:
+            nc.scalar.copy(out=singles[:, :, t0:t1], in_=singles_raw[:, :, t0:t1])
+
+        def listed(experts):
+            return offsets[:, experts[0] * C // 16 : (experts[-1] + 1) * C // 16]
 
         def prepare(u):
             experts = UNITS[u]
-            count = len(experts)
-            slots = count * C
+            slots = len(experts) * C
             first = experts[0] * C
-            listed = offsets[:, first // 16 : (first + slots) // 16]
-            g = grouped[:, first : first + slots, :]
+            group = grouped[:, first : first + slots, :]
             for j in range(2):
-                if u in (0,):
-                    nc.vector.tensor_copy(out=g[:, :, 2 + j], in_=late_raw[:, j, :].indirect(listed))
+                if u == 0:
+                    nc.vector.tensor_copy(out=group[:, :, 2 + j], in_=singles_raw[:, j, :].indirect(listed(experts)))
                 else:
-                    nc.scalar.activation(out=g[:, :, 2 + j], in_=late[:, j, :].indirect(listed), func=COPY)
-            xc = keep.tile([P, slots], U32, name=f"x_codes{u}", align_bytes=64)
-            xb = keep.tile([P, slots], U8, name=f"x_bytes{u}", align_bytes=64)
-            nc.vector.quantize_mx(out=xc[:].bitcast(FP8X4), scales=xb[:], in_=g.rearrange("p n j -> p (n j)"))
+                    nc.scalar.activation(out=group[:, :, 2 + j], in_=singles[:, j, :].indirect(listed(experts)), func=COPY)
+            x_codes = keep.tile([P, slots], U32, name=f"x_codes{u}", align_bytes=64)
+            x_scales = keep.tile([P, slots], U8, name=f"x_scales{u}", align_bytes=64)
+            nc.vector.quantize_mx(out=x_codes[:].bitcast(FP8X4), scales=x_scales[:], in_=flat(group))
 
-            wg = keep.tile([P, count * N, PACK], BF16, name=f"w_grouped{u}", align_bytes=64)
-            for h, e, n0, n1 in ((0, 0, 0, P), (0, 0, P, N)) if u == 0 else [(h, e, 0, N) for h, e in enumerate(experts)]:
-                interleave(w_copy[e], wg[:, h * N + n0 : h * N + n1, :], w_raw[e][:, :, n0:n1])
-            wc = keep.tile([P, count * N], U32, name=f"w_codes{u}", align_bytes=64)
-            wb = keep.tile([P, count * N], U8, name=f"w_bytes{u}", align_bytes=64)
-            for c0, n in ((0, P), (P, 2 * P)) if u == 0 else ((0, count * 256), (count * 256, count * 128)):
+            features = len(experts) * N
+            w_grouped = keep.tile([P, features, PACK], BF16, name=f"w_grouped{u}", align_bytes=64)
+            w_codes = keep.tile([P, features], U32, name=f"w_codes{u}", align_bytes=64)
+            w_scales = keep.tile([P, features], U8, name=f"w_scales{u}", align_bytes=64)
+            if u == 0:
+                copied = quantised = (0, P, N)
+            else:
+                copied = tuple(range(0, features + 1, N))
+                quantised = (0, 2 * features // 3, features)
+            for n0, n1 in zip(copied, copied[1:]):
+                raw = w_raw[experts[n0 // N]]
+                n_in = n0 % N
+                interleave(nc.scalar.copy, w_grouped[:, n0:n1, :], raw[:, :, n_in : n_in + n1 - n0])
+            for n0, n1 in zip(quantised, quantised[1:]):
                 nc.vector.quantize_mx(
-                    out=wc[:, c0 : c0 + n].bitcast(FP8X4),
-                    scales=wb[:, c0 : c0 + n],
-                    in_=wg[:, c0 : c0 + n, :].rearrange("p n j -> p (n j)"),
+                    out=w_codes[:, n0:n1].bitcast(FP8X4),
+                    scales=w_scales[:, n0:n1],
+                    in_=flat(w_grouped[:, n0:n1, :]),
                 )
-            return xc, xb, wc, wb
+            return x_codes, x_scales, w_codes, w_scales
 
-        def compute(u, xc, xb, wc, wb):
+        def multiply(u, x_codes, x_scales, w_codes, w_scales):
             experts = UNITS[u]
             slots = len(experts) * C
             first = experts[0] * C
-            listed = offsets[:, first // 16 : (first + slots) // 16]
-            for m in range(M_TILES):
-                acc = psum.tile([P, 512], F32, name="acc")
-                y = work.tile([P, 512], F32, name="y")
+            gates = gate_first[:] if u == 0 else gate_rest[:, first - C : first - C + slots]
+            for m in range(BLOCKS):
+                acc = psum.tile([P, BANK], F32, name="acc")
+                y = results.tile([P, BANK], F32, name="y")
                 for h, e in enumerate(experts):
                     cols = slice(h * C, (h + 1) * C)
                     feats = slice(h * N + m * P, h * N + (m + 1) * P)
                     nc.tensor.matmul_mx(
                         out=acc[:, cols],
-                        lhsT=wc[:, feats].bitcast(FP8X4),
-                        lhsT_scale=wb[:, feats],
-                        rhs=xc[:, cols].bitcast(FP8X4),
-                        rhs_scale=xb[:, cols],
+                        lhsT=w_codes[:, feats].bitcast(FP8X4),
+                        lhsT_scale=w_scales[:, feats],
+                        rhs=x_codes[:, cols].bitcast(FP8X4),
+                        rhs_scale=x_scales[:, cols],
                         start=True,
                         stop=True,
                     )
                     nc.scalar.activation(out=y[:, cols], in_=acc[:, cols], func=SILU, bias=bias[:, m, e : e + 1])
                 nc.vector.tensor_tensor(
-                    out=windows[m][:].indirect(listed),
-                    in0=y[:, 0:slots],
-                    in1=gate_first[:] if u == 0 else gate_rest[:, first - C : first - C + slots],
-                    op=MULT,
+                    out=windows[m][:].indirect(listed(experts)), in0=y[:, 0:slots], in1=gates, op=MULT
                 )
                 if u == len(UNITS) - 1:
                     nc.sync.dma_start(out=out[m * P : (m + 1) * P, :], in_=windows[m][:])
 
-        ready = [prepare(0)]
+        ready = prepare(0)
         for u in range(len(UNITS)):
+            current = ready
             if u + 1 < len(UNITS):
-                ready.append(prepare(u + 1))
-            compute(u, *ready[u])
+                ready = prepare(u + 1)
+            multiply(u, *current)

from contextlib import ExitStack

import concourse.mybir as mybir

K, T, E, C, N = 512, 2048, 6, 256, 384
FLOPS = 2 * K * N * E * C
BYTES = 4 * (K * T + E * K * N + N * E + E * C + N * T) + 2 * 128 * (E * C // 16)

F32 = mybir.dt.float32
BF16 = mybir.dt.bfloat16
U32 = mybir.dt.uint32
U16 = mybir.dt.uint16
U8 = mybir.dt.uint8
FP8X4 = mybir.dt.float8_e4m3fn_x4
MULT = mybir.AluOpType.mult
SILU = mybir.ActivationFunctionType.Silu
COPY = mybir.ActivationFunctionType.Copy

P = 128
PACK = 4
BLOCKS = N // P
BANK = 512
BANKS = 8

UNITS = ((0,), (1,), (2,), (3,), (4, 5))
PAIR_LOADS = ((0, 1024), (1024, 1536), (1536, 2048))
SINGLE_LOADS = ((0, 1024), (1024, 2048))
SINGLE_COPIES = ((0, 512), (512, 1024), (1024, 1536), (1536, 2048))
RESULT_BUFS = 12


def interleave(copy, out, raw):
    copy(out=out.rearrange("p (c i) j -> p c j i", i=4), in_=raw.rearrange("p j (c i) -> p c j i", i=4))


def flat(tile_view):
    return tile_view.rearrange("p n j -> p (n j)")


def tile_routed_moe_kernel(tc, xT, w, b, gate, offs, out):
    nc = tc.nc
    with ExitStack() as ctx:
        keep = ctx.enter_context(tc.tile_pool(name="keep", bufs=1))
        results = ctx.enter_context(tc.tile_pool(name="results", bufs=RESULT_BUFS))
        psum = ctx.enter_context(tc.psum_pool(name="psum", bufs=BANKS))

        offsets = keep.tile([P, E * C // 16], U16, name="offsets")
        bias = keep.tile([P, BLOCKS, E], F32, name="bias")
        gate_first = keep.tile([P, C], F32, name="gate_first")
        gate_rest = keep.tile([P, (E - 1) * C], F32, name="gate_rest")
        windows = [keep.tile([P, T], F32, name=f"window{m}") for m in range(BLOCKS)]
        warm = keep.tile([P, 1], F32, name="warm")
        pairs = keep.tile([P, T, 2], BF16, name="pairs", align_bytes=64)
        singles = keep.tile([P, 2, T], BF16, name="singles", align_bytes=64)
        singles_raw = keep.tile([P, 2, T], F32, name="singles_raw")
        grouped = keep.tile([P, E * C, PACK], BF16, name="grouped", align_bytes=64)

        x_rows = xT.rearrange("(p j) t -> p j t", j=PACK)
        pairs_raw, w_raw = [], []
        for c, (t0, t1) in enumerate(PAIR_LOADS):
            raw = keep.tile([P, 2, t1 - t0], F32, name=f"pairs_raw{c}")
            nc.sync.dma_start(out=raw[:], in_=x_rows[:, 0:2, t0:t1])
            pairs_raw.append(raw)
            if c == 0:
                nc.sync.dma_start(offsets[:], offs)
        for t0, t1 in SINGLE_LOADS:
            nc.sync.dma_start(out=singles_raw[:, :, t0:t1], in_=x_rows[:, 2:4, t0:t1])
        for e in range(E):
            raw = keep.tile([P, PACK, N], F32, name=f"w_raw{e}")
            nc.sync.dma_start(out=raw[:], in_=w[e].rearrange("(p j) n -> p j n", j=PACK))
            w_raw.append(raw)
            if e == 0:
                nc.sync.dma_start(out=bias[:], in_=b.rearrange("(m p) e -> p m e", p=P))
                nc.sync.dma_start(out=gate_first[:], in_=gate[0:P, 0:C])
            if e == 1:
                nc.sync.dma_start(out=gate_rest[:], in_=gate[0:P, C:])

        nc.vector.memset(warm[:], 0.0)
        nc.scalar.activation(out=warm[:], in_=warm[:], func=SILU)
        nc.vector.memset(windows[0][:], 0.0)
        nc.vector.memset(windows[1][:], 0.0)
        nc.gpsimd.memset(windows[2][:], 0.0)

        for (t0, t1), raw in zip(PAIR_LOADS, pairs_raw):
            interleave(nc.vector.tensor_copy, pairs[:, t0:t1, :], raw[:])
        nc.vector.tensor_copy(
            out=flat(grouped[:]).bitcast(U32).rearrange("p (n u) -> p n u", u=2)[:, :, 0],
            in_=flat(pairs[:]).bitcast(U32).indirect(offsets[:]),
        )
        for t0, t1 in SINGLE_COPIES:
            nc.scalar.copy(out=singles[:, :, t0:t1], in_=singles_raw[:, :, t0:t1])

        def listed(experts):
            return offsets[:, experts[0] * C // 16 : (experts[-1] + 1) * C // 16]

        def prepare(u):
            experts = UNITS[u]
            slots = len(experts) * C
            first = experts[0] * C
            group = grouped[:, first : first + slots, :]
            for j in range(2):
                if u == 0:
                    nc.vector.tensor_copy(out=group[:, :, 2 + j], in_=singles_raw[:, j, :].indirect(listed(experts)))
                else:
                    nc.scalar.activation(out=group[:, :, 2 + j], in_=singles[:, j, :].indirect(listed(experts)), func=COPY)
            x_codes = keep.tile([P, slots], U32, name=f"x_codes{u}", align_bytes=64)
            x_scales = keep.tile([P, slots], U8, name=f"x_scales{u}", align_bytes=64)
            nc.vector.quantize_mx(out=x_codes[:].bitcast(FP8X4), scales=x_scales[:], in_=flat(group))

            features = len(experts) * N
            w_grouped = keep.tile([P, features, PACK], BF16, name=f"w_grouped{u}", align_bytes=64)
            w_codes = keep.tile([P, features], U32, name=f"w_codes{u}", align_bytes=64)
            w_scales = keep.tile([P, features], U8, name=f"w_scales{u}", align_bytes=64)
            if u == 0:
                copied = quantised = (0, P, N)
            else:
                copied = tuple(range(0, features + 1, N))
                quantised = (0, 2 * features // 3, features)
            for n0, n1 in zip(copied, copied[1:]):
                raw = w_raw[experts[n0 // N]]
                n_in = n0 % N
                interleave(nc.scalar.copy, w_grouped[:, n0:n1, :], raw[:, :, n_in : n_in + n1 - n0])
            for n0, n1 in zip(quantised, quantised[1:]):
                nc.vector.quantize_mx(
                    out=w_codes[:, n0:n1].bitcast(FP8X4),
                    scales=w_scales[:, n0:n1],
                    in_=flat(w_grouped[:, n0:n1, :]),
                )
            return x_codes, x_scales, w_codes, w_scales

        def multiply(u, x_codes, x_scales, w_codes, w_scales):
            experts = UNITS[u]
            slots = len(experts) * C
            first = experts[0] * C
            gates = gate_first[:] if u == 0 else gate_rest[:, first - C : first - C + slots]
            for m in range(BLOCKS):
                acc = psum.tile([P, BANK], F32, name="acc")
                y = results.tile([P, BANK], F32, name="y")
                for h, e in enumerate(experts):
                    cols = slice(h * C, (h + 1) * C)
                    feats = slice(h * N + m * P, h * N + (m + 1) * P)
                    nc.tensor.matmul_mx(
                        out=acc[:, cols],
                        lhsT=w_codes[:, feats].bitcast(FP8X4),
                        lhsT_scale=w_scales[:, feats],
                        rhs=x_codes[:, cols].bitcast(FP8X4),
                        rhs_scale=x_scales[:, cols],
                        start=True,
                        stop=True,
                    )
                    nc.scalar.activation(out=y[:, cols], in_=acc[:, cols], func=SILU, bias=bias[:, m, e : e + 1])
                nc.vector.tensor_tensor(
                    out=windows[m][:].indirect(listed(experts)), in0=y[:, 0:slots], in1=gates, op=MULT
                )
                if u == len(UNITS) - 1:
                    nc.sync.dma_start(out=out[m * P : (m + 1) * P, :], in_=windows[m][:])

        ready = prepare(0)
        for u in range(len(UNITS)):
            current = ready
            if u + 1 < len(UNITS):
                ready = prepare(u + 1)
            multiply(u, *current)
